import numpy as np, ml_dtypes
CORES = [0,1,2,3,4,5,6,7]
N = 8
def setup_inputs(rng):
    return {"x": rng.standard_normal((N, 128, 1024), dtype=np.float32).astype(ml_dtypes.bfloat16)}
def reference(x):
    s = x.sum(axis=0, dtype=np.float64).astype(x.dtype)
    p = 128 // N
    return {"y": np.stack([s[r * p:(r + 1) * p, :] for r in range(N)])}

@@ -1,0 +1,46 @@
+from concourse.bass import DstId, RemoteDMATransfer
+
+N = 8
+SCRATCH = {
+    "stage": ("dram", [N, 128, 128], "bfloat16"),
+    "land": ("dram", [N, 128, 128], "bfloat16"),
+    "res": ("dram", [128, 128], "bfloat16"),
+}
+SEMAPHORES = ["loaded", "sent", "arrived", "done", "stored"]
+
+
+def rank_program(g, core, T, topo):
+    r = T.rank_of(core)
+    if r is None:
+        return
+    cores = T.cores
+
+    def dst_id(c):
+        rid, pid, _se = topo.addr(c)
+        return DstId(rid=rid, pnc=pid)
+
+    g.sync.dma_start(T.stage[:], T.x[:]).then_inc(T.sem.loaded, 16)
+    g.wait_ge(T.sem.loaded, 16)
+
+    mine = r ^ 1
+    trs = []
+    k = 0
+    for d in range(N):
+        if d == mine:
+            continue
+        trs.append(RemoteDMATransfer(dst_ids=[dst_id(cores[d ^ 1])], dma_engine_mask=0x3 << (2 * k),
+                                     remote_sem=T.sem.arrived, src=T.stage[d], dst=T.land[r]))
+        k += 1
+    g.remote_dma_fused(trs, local_sem=T.sem.sent)
+
+    g.wait_ge(T.sem.arrived, 14)
+    srcs = [T.land[s] for s in range(N) if s != r] + [T.stage[mine]]
+    g.remote_dma_fused([RemoteDMATransfer(dst_ids=[dst_id(cores[mine])], dma_engine_mask=0xFFFF,
+                                          remote_sem=T.sem.done, srcs=srcs, dsts=[T.res[:]], alu_op=1)],
+                       local_sem=T.sem.sent)
+
+    g.wait_ge(T.sem.done, 16)
+    g.sync.wait_ge(T.sem.done, 16)
+    g.sync.dma_start(T.y[:], T.res[:]).then_inc(T.sem.stored, 16)
+    g.wait_ge(T.sem.stored, 16)
+    g.wait_ge(T.sem.sent, 30)

@@ -1,12 +1,13 @@
 from concourse.bass import DstId, RemoteDMATransfer
+from concourse.mybir import AluOpType
 
 N = 8
 SCRATCH = {
     "stage": ("dram", [N, 128, 128], "bfloat16"),
-    "land": ("dram", [N, 128, 128], "bfloat16"),
+    "land": ("dram", [N - 2, 128, 128], "bfloat16"),
     "res": ("dram", [128, 128], "bfloat16"),
 }
-SEMAPHORES = ["loaded", "sent", "arrived", "done", "stored"]
+SEMAPHORES = ["loaded", "seeded", "sent", "arrived", "done", "stored"]
 
 
 def rank_program(g, core, T, topo):
@@ -14,33 +15,34 @@ def rank_program(g, core, T, topo):
     if r is None:
         return
     cores = T.cores
+    p = 128 // N
+    nb = r ^ 1
 
     def dst_id(c):
         rid, pid, _se = topo.addr(c)
         return DstId(rid=rid, pnc=pid)
 
     g.sync.dma_start(T.stage[:], T.x[:]).then_inc(T.sem.loaded, 16)
+    g.scalar.dma_start(T.y[:], T.x[r * p:(r + 1) * p, :]).then_inc(T.sem.seeded, 16)
     g.wait_ge(T.sem.loaded, 16)
 
-    mine = r ^ 1
     trs = []
-    k = 0
     for d in range(N):
-        if d == mine:
+        if d in (r, nb):
             continue
-        trs.append(RemoteDMATransfer(dst_ids=[dst_id(cores[d ^ 1])], dma_engine_mask=0x3 << (2 * k),
-                                     remote_sem=T.sem.arrived, src=T.stage[d], dst=T.land[r]))
-        k += 1
+        slot = r if r < (d & ~1) else r - 2
+        trs.append(RemoteDMATransfer(dst_ids=[dst_id(cores[d ^ 1])], dma_engine_mask=0x3 << (2 * len(trs)),
+                                     remote_sem=T.sem.arrived, src=T.stage[d], dst=T.land[slot]))
     g.remote_dma_fused(trs, local_sem=T.sem.sent)
 
-    g.wait_ge(T.sem.arrived, 14)
-    srcs = [T.land[s] for s in range(N) if s != r] + [T.stage[mine]]
-    g.remote_dma_fused([RemoteDMATransfer(dst_ids=[dst_id(cores[mine])], dma_engine_mask=0xFFFF,
+    g.wait_ge(T.sem.arrived, 2 * (N - 2))
+    srcs = [T.land[k] for k in range(N - 2)] + [T.stage[nb]]
+    g.remote_dma_fused([RemoteDMATransfer(dst_ids=[dst_id(cores[nb])], dma_engine_mask=topo.mask(core, cores[nb]),
                                           remote_sem=T.sem.done, srcs=srcs, dsts=[T.res[:]], alu_op=1)],
                        local_sem=T.sem.sent)
 
+    g.wait_ge(T.sem.seeded, 16)
     g.wait_ge(T.sem.done, 16)
-    g.sync.wait_ge(T.sem.done, 16)
-    g.sync.dma_start(T.y[:], T.res[:]).then_inc(T.sem.stored, 16)
+    g.dma_start(T.y[:], T.res[:], accum_op=AluOpType.add, max_dma_last_dim=4096).then_inc(T.sem.stored, 16)
     g.wait_ge(T.sem.stored, 16)
-    g.wait_ge(T.sem.sent, 30)
+    g.wait_ge(T.sem.sent, 2 * (N - 2) + 16)

from concourse.bass import DstId, RemoteDMATransfer
from concourse.mybir import AluOpType

N = 8
SCRATCH = {
    "stage": ("dram", [N, 128, 128], "bfloat16"),
    "land": ("dram", [N - 2, 128, 128], "bfloat16"),
    "res": ("dram", [128, 128], "bfloat16"),
}
SEMAPHORES = ["loaded", "seeded", "sent", "arrived", "done", "stored"]


def rank_program(g, core, T, topo):
    r = T.rank_of(core)
    if r is None:
        return
    cores = T.cores
    p = 128 // N
    nb = r ^ 1

    def dst_id(c):
        rid, pid, _se = topo.addr(c)
        return DstId(rid=rid, pnc=pid)

    g.sync.dma_start(T.stage[:], T.x[:]).then_inc(T.sem.loaded, 16)
    g.scalar.dma_start(T.y[:], T.x[r * p:(r + 1) * p, :]).then_inc(T.sem.seeded, 16)
    g.wait_ge(T.sem.loaded, 16)

    trs = []
    for d in range(N):
        if d in (r, nb):
            continue
        slot = r if r < (d & ~1) else r - 2
        trs.append(RemoteDMATransfer(dst_ids=[dst_id(cores[d ^ 1])], dma_engine_mask=0x3 << (2 * len(trs)),
                                     remote_sem=T.sem.arrived, src=T.stage[d], dst=T.land[slot]))
    g.remote_dma_fused(trs, local_sem=T.sem.sent)

    g.wait_ge(T.sem.arrived, 2 * (N - 2))
    srcs = [T.land[k] for k in range(N - 2)] + [T.stage[nb]]
    g.remote_dma_fused([RemoteDMATransfer(dst_ids=[dst_id(cores[nb])], dma_engine_mask=topo.mask(core, cores[nb]),
                                          remote_sem=T.sem.done, srcs=srcs, dsts=[T.res[:]], alu_op=1)],
                       local_sem=T.sem.sent)

    g.wait_ge(T.sem.seeded, 16)
    g.wait_ge(T.sem.done, 16)
    g.dma_start(T.y[:], T.res[:], accum_op=AluOpType.add, max_dma_last_dim=4096).then_inc(T.sem.stored, 16)
    g.wait_ge(T.sem.stored, 16)
    g.wait_ge(T.sem.sent, 2 * (N - 2) + 16)
